import numpy as np
import ml_dtypes


def mxq(x, axis, fmt="e4m3"):
    dtype, down = {"e4m3": (ml_dtypes.float8_e4m3fn, 7), "e5m2": (ml_dtypes.float8_e5m2, 14)}[fmt]
    v = np.moveaxis(np.asarray(x, np.float32).astype(ml_dtypes.bfloat16).astype(np.float64), axis, -1)
    blocks = v.reshape(v.shape[:-1] + (-1, 32))
    amax = np.abs(blocks).max(-1, keepdims=True)
    byte = np.maximum(np.where(amax > 0, np.frexp(amax)[1] - 1 + 127, 0) - down, 1)
    scale = np.exp2(byte - 127.0)
    codes = (blocks / scale).astype(np.float32).astype(dtype).astype(np.float64)
    return np.moveaxis((codes * scale).reshape(v.shape), -1, axis)


WIDE = False


def mx_kscale(k):
    if not WIDE:
        return np.ones(k)
    levels = np.array([10, -10, 5, -5, 0])
    if k % 512:
        return np.exp2(np.random.permutation(np.resize(levels, k // 32))).repeat(32)
    a = np.empty((k // 512, 16))
    for p in range(k // 512):
        a[p, :8] = np.random.permutation(np.resize(levels, 8))
        for g in range(8):
            far = levels[np.abs(levels - a[p, g]) >= 10]
            a[p, g + 8] = far[np.random.randint(len(far))]
    return np.exp2(a.ravel()).repeat(32)


BF16 = ml_dtypes.bfloat16


def bf(x):
    return np.asarray(x, np.float32).astype(BF16)


def f64(x):
    return np.asarray(x).astype(np.float64)


B, I, J, P, Q = 16, 512, 1024, 256, 128


def silu(v):
    return v / (1.0 + np.exp(-v))


def two_sided(xq, a, b):
    t = xq @ mxq(f64(b), 0, "e4m3")
    return mxq(f64(a), 1, "e4m3") @ mxq(t, 1, "e4m3")


def draw0():
    s, u = mx_kscale(J), mx_kscale(I)
    x = np.random.standard_normal((B, I, J)) * s[None, None, :] * u[None, :, None]
    b1 = np.random.standard_normal((J, Q)) / np.sqrt(J) / s[:, None]
    b2 = np.random.standard_normal((J, Q)) / np.sqrt(J) / s[:, None]
    a1 = np.random.standard_normal((P, I)) / np.sqrt(I) / u[None, :]
    a2 = np.random.standard_normal((P, I)) / np.sqrt(I) / u[None, :]
    c = 0.5 * np.random.standard_normal((P, Q))
    return {"x": bf(x), "b1": bf(b1), "b2": bf(b2), "a1": bf(a1), "a2": bf(a2), "c": bf(c)}


def core(x, b1, b2, a1, a2, c):
    xq = mxq(f64(x), 2, "e4m3")
    u1 = two_sided(xq, a1, b1)
    u2 = two_sided(xq, a2, b2)
    z = u1 + u2 + f64(c)[None, :, :]
    return silu(z)


def e4m3fn_bytes(y):
    return np.clip(np.asarray(y, np.float64), -448.0, 448.0).astype(np.float32).astype(ml_dtypes.float8_e4m3fn).view(np.uint8)


def e4m3fn_values(b):
    return np.asarray(b, np.uint8).view(ml_dtypes.float8_e4m3fn).astype(np.float64)


def setup_inputs():
    d = draw0()
    x0 = np.asarray(d['b2']).astype(np.float64)
    s = (np.max(np.abs(x0), axis=(1,), keepdims=True) / 448.0).astype(np.float32)
    out = {}
    for k, v in d.items():
        if k == 'b2':
            out['b2_bytes'] = e4m3fn_bytes(x0 / s.astype(np.float64))
            out['b2_scale'] = s
        else:
            out[k] = v
    return out


def reference(x, b1, b2_bytes, b2_scale, a1, a2, c):
    return core(x, b1, e4m3fn_values(b2_bytes) * b2_scale.astype(np.float64), a1, a2, c)

@@ -1,0 +1,333 @@
+from contextlib import ExitStack
+
+import concourse.mybir as mybir
+from concourse.masks import make_identity
+
+FLOPS = 2 * 16 * 512 * 1024 * 256 + 2 * 2 * 16 * 256 * 512 * 128
+
+P = 128
+NB = 16
+F32 = mybir.dt.float32
+BF16 = mybir.dt.bfloat16
+U32 = mybir.dt.uint32
+U8 = mybir.dt.uint8
+FP8 = mybir.dt.float8_e4m3fn
+FP8X4 = mybir.dt.float8_e4m3fn_x4
+ACT = mybir.ActivationFunctionType
+ALU = mybir.AluOpType
+
+X_BUFS = 16
+
+
+def tile_ranktwokroneckersumlayer_t_kernel(tc, x, b1, b2_bytes, b2_scale, a1, a2, c, out):
+    nc = tc.nc
+
+    def permuted_slots(n):
+        return (0, 2)[n] if n < 2 else (4 if n % 2 else 3)
+
+    with ExitStack() as ctx:
+        keep = ctx.enter_context(tc.tile_pool(name="keep", bufs=1))
+        xpool = ctx.enter_context(tc.tile_pool(name="xpool", bufs=X_BUFS))
+        ppool = ctx.enter_context(tc.tile_pool(name="ppool", bufs=2))
+        gpool = ctx.enter_context(tc.tile_pool(name="gpool", bufs=4))
+        qpool = ctx.enter_context(tc.tile_pool(name="qpool", bufs=6))
+        tpool = ctx.enter_context(tc.tile_pool(name="tpool", bufs=2))
+        zpool = ctx.enter_context(tc.tile_pool(name="zpool", bufs=3))
+        ps_t = ctx.enter_context(tc.psum_pool(name="ps_t", bufs=4))
+        ps_s = ctx.enter_context(tc.psum_pool(name="ps_s", bufs=3))
+        ps_z = ctx.enter_context(tc.psum_pool(name="ps_z", bufs=1))
+        ctx.enter_context(tc.manual_schedule())
+
+        ident = keep.tile([P, P], F32, name="ident")
+        warm = keep.tile([P, 1], F32, name="warm")
+        b2_raw = keep.tile([P, 2, 4, P], U8, name="b2_raw")
+        b2_s = keep.tile([P, 2, 4], F32, name="b2_s")
+        b2_w = keep.tile([P, 2, 4, P], BF16, name="b2_w")
+        b1_raw = keep.tile([P, 2, 4, P], BF16, name="b1_raw")
+        b_grp = keep.tile([P, 2 * 1024], BF16, name="b_grp", align_bytes=64)
+        b_codes = keep.tile([P, 512], U32, name="b_codes", align_bytes=64)
+        b_scales = keep.tile([P, 512], U8, name="b_scales", align_bytes=64)
+        a_raw = keep.tile([P, 2, 1024], BF16, name="a_raw")
+        a_grp = keep.tile([P, 2048], BF16, name="a_grp", align_bytes=64)
+        a_codes = keep.tile([P, 512], U32, name="a_codes", align_bytes=64)
+        a_scales = keep.tile([P, 512], U8, name="a_scales", align_bytes=64)
+        c_t = keep.tile([P, 2, 256], BF16, name="c_t")
+
+        xs = {}
+
+        loaded = {}
+
+        def load_x(n, pieces=(4,)):
+            if n not in xs:
+                xs[n] = xpool.tile([P, 4, 1024], BF16, name="x_t")
+            src = x[n].rearrange("(m s) k -> m s k", s=4)
+            for step in pieces:
+                s = loaded.get(n, 0)
+                nc.sync.dma_start(out=xs[n][:, s : s + step, :], in_=src[:, s : s + step, :])
+                loaded[n] = s + step
+
+        nc.sync.dma_start(out=b2_s[:], in_=b2_scale.rearrange("(g p t) o -> p g (t o)", g=2, t=4))
+        nc.sync.dma_start(out=b2_raw[:], in_=b2_bytes.rearrange("(g p t) q -> p g t q", g=2, t=4))
+        load_x(0, (1,))
+        nc.sync.dma_start(out=b1_raw[:], in_=b1.rearrange("(g p t) q -> p g t q", g=2, t=4))
+        load_x(0, (1, 1, 1))
+        load_x(1, (2, 2))
+        nc.sync.dma_start(out=a_raw[:, 0, :], in_=a1.rearrange("(m h) k -> m (h k)", h=2))
+        nc.sync.dma_start(out=a_raw[:, 1, :], in_=a2.rearrange("(m h) k -> m (h k)", h=2))
+        for i in range(2):
+            nc.sync.dma_start(out=c_t[:, i, :], in_=c.rearrange("(m h) q -> m (h q)", h=2))
+        for n in range(2, X_BUFS):
+            load_x(n)
+
+        nc.gpsimd.memset(warm[:], 0.0)
+        make_identity(nc, ident[:])
+        nc.scalar.activation(out=warm[:], in_=warm[:], func=ACT.Silu)
+
+        for i in range(8):
+            g, t = divmod(i, 4)
+            src = b2_raw[:, g, t, :].bitcast(FP8)
+            if i < 3:
+                nc.vector.tensor_scalar(
+                    out=b2_w[:, g, t, :], in0=src, scalar1=b2_s[:, g, t : t + 1], scalar2=None, op0=ALU.mult
+                )
+            else:
+                nc.scalar.activation(out=b2_w[:, g, t, :], in_=src, func=ACT.Copy, scale=b2_s[:, g, t : t + 1])
+
+        def interleave_b(i, src):
+            nc.vector.tensor_copy(
+                out=b_grp[:, 1024 * i : 1024 * (i + 1)].rearrange("p (g q t) -> p g q t", g=2, t=4),
+                in_=src[:].rearrange("p g t q -> p g q t"),
+            )
+
+        def quantize_b(i):
+            nc.vector.quantize_mx(
+                out=b_codes[:, 256 * i : 256 * (i + 1)].bitcast(FP8X4),
+                scales=b_scales[:, 256 * i : 256 * (i + 1)],
+                in_=b_grp[:, 1024 * i : 1024 * (i + 1)],
+            )
+
+        perm = {}
+        banks = {}
+        grp = {}
+        codes = {}
+        s1 = {}
+        tg = {}
+        tcodes = {}
+        zb = {}
+        zs = {}
+
+        def permute(n):
+            k = permuted_slots(n)
+            if k == 0:
+                return
+            t = ppool.tile([P, 4096], BF16, name="x_p")
+            nc.vector.tensor_copy(
+                out=t[:, : 1024 * k].bitcast(F32).rearrange("p (a u w) -> p a u w", u=2, w=P),
+                in_=xs[n][:, :k, :].rearrange("p s k -> p (s k)").bitcast(F32).rearrange("p (a w u) -> p a u w", u=2, w=P),
+            )
+            perm[n] = t
+
+        def transposes(n, s):
+            bank = ps_t.tile([P, 4, P], F32, name="t_bank")
+            for g in range(2):
+                for u in range(2):
+                    if s < permuted_slots(n):
+                        w = perm[n][:].bitcast(F32)
+                        lo = 512 * s + 256 * g + 128 * u
+                        src = w[:, lo : lo + 128]
+                    else:
+                        w = xs[n][:, s, :].bitcast(F32)
+                        src = w[:, 256 * g + u : 256 * (g + 1) : 2]
+                    nc.tensor.transpose(bank[:, 2 * g + u, :], src, ident[:])
+            banks[n, s] = bank
+
+        def unload(n, s, eng):
+            h, s2 = divmod(s, 2)
+            if s2 == 0:
+                grp[n, h] = gpool.tile([P, 2048], BF16, name="x_g", align_bytes=64)
+            dst = grp[n, h][:].bitcast(F32)[:, 512 * s2 : 512 * (s2 + 1)].rearrange("p (g m u) -> p g m u", g=2, u=2)
+            src = banks[n, s][:].rearrange("p (g u) m -> p g m u", g=2)
+            if eng == "S":
+                nc.scalar.copy(out=dst, in_=src)
+            else:
+                nc.vector.tensor_copy(out=dst, in_=src)
+
+        def quantize_x(n, h):
+            q = qpool.tile([P, 512], U32, name="x_q", align_bytes=64)
+            sc = qpool.tile([P, 512], U8, name="x_s", align_bytes=64)
+            nc.vector.quantize_mx(out=q[:].bitcast(FP8X4), scales=sc[:], in_=grp[n, h][:])
+            codes[n, h] = (q, sc)
+
+        def stage1(n, b):
+            bank = ps_s.tile([P, 4, P], F32, name="s_bank")
+            for t in range(4):
+                q, sc = codes[n, t // 2]
+                for g in range(2):
+                    cols = slice(256 * (t % 2) + 128 * g, 256 * (t % 2) + 128 * (g + 1))
+                    bcols = slice(256 * b + 128 * g, 256 * b + 128 * (g + 1))
+                    nc.tensor.matmul_mx(
+                        out=bank[:, t, :],
+                        lhsT=q[:, cols].bitcast(FP8X4),
+                        lhsT_scale=sc[:, cols],
+                        rhs=b_codes[:, bcols].bitcast(FP8X4),
+                        rhs_scale=b_scales[:, bcols],
+                        start=(g == 0),
+                        stop=(g == 1),
+                    )
+            s1[n, b] = bank
+
+        def unload1(n, b, eng):
+            pair, i = divmod(n, 2)
+            if i == 0 and b == 0:
+                tg[pair] = tpool.tile([P, 2048], BF16, name="t_g", align_bytes=64)
+            lo = 512 * (2 * b + i)
+            dst = tg[pair][:, lo : lo + 512].rearrange("p (q t) -> p q t", t=4)
+            src = s1[n, b][:].rearrange("p t q -> p q t")
+            if eng == "S":
+                nc.scalar.copy(out=dst, in_=src)
+            else:
+                nc.vector.tensor_copy(out=dst, in_=src)
+
+        def quantize_t_one(n):
+            pair, i = divmod(n, 2)
+            if i == 0:
+                q = tpool.tile([P, 512], U32, name="t_q", align_bytes=64)
+                sc = tpool.tile([P, 512], U8, name="t_s", align_bytes=64)
+                tcodes[pair] = (q, sc)
+            q, sc = tcodes[pair]
+            for b in range(2):
+                lo = 128 * (2 * b + i)
+                nc.vector.quantize_mx(
+                    out=q[:, lo : lo + 128].bitcast(FP8X4), scales=sc[:, lo : lo + 128], in_=tg[pair][:, 4 * lo : 4 * lo + 512]
+                )
+
+        def stage2_one(n):
+            pair, i = divmod(n, 2)
+            bank = ps_t.tile([P, 4, P], F32, name="t_bank")
+            q, sc = tcodes[pair]
+            for h in range(2):
+                for b in range(2):
+                    acols = slice(128 * (2 * b + h), 128 * (2 * b + h + 1))
+                    tcols = slice(128 * (2 * b + i), 128 * (2 * b + i + 1))
+                    nc.tensor.matmul_mx(
+                        out=bank[:, h, :],
+                        lhsT=a_codes[:, acols].bitcast(FP8X4),
+                        lhsT_scale=a_scales[:, acols],
+                        rhs=q[:, tcols].bitcast(FP8X4),
+                        rhs_scale=sc[:, tcols],
+                        start=(b == 0),
+                        stop=(b == 1),
+                    )
+            zb[n, "one"] = bank
+
+        def finish_one(n):
+            t = zpool.tile([P, 2, P], F32, name="z_one")
+            nc.vector.tensor_tensor(
+                out=t[:], in0=zb[n, "one"][:, :2, :], in1=c_t[:, 0, :].rearrange("p (h q) -> p h q", h=2), op=ALU.add
+            )
+            o = zpool.tile([P, 2, P], F32, name="o_one")
+            nc.scalar.activation(out=o[:], in_=t[:], func=ACT.Silu)
+            nc.sync.dma_start(out=out[n].rearrange("(m h) q -> m (h q)", h=2), in_=o[:].rearrange("p h q -> p (h q)"))
+
+        def quantize_t(pair):
+            q = tpool.tile([P, 512], U32, name="t_q", align_bytes=64)
+            sc = tpool.tile([P, 512], U8, name="t_s", align_bytes=64)
+            nc.vector.quantize_mx(out=q[:].bitcast(FP8X4), scales=sc[:], in_=tg[pair][:])
+            tcodes[pair] = (q, sc)
+
+        def stage2(pair):
+            bank = ps_z.tile([P, 2, 256], F32, name="z_bank")
+            q, sc = tcodes[pair]
+            for h in range(2):
+                for b in range(2):
+                    acols = slice(128 * (2 * b + h), 128 * (2 * b + h + 1))
+                    tcols = slice(256 * b, 256 * (b + 1))
+                    nc.tensor.matmul_mx(
+                        out=bank[:, h, :],
+                        lhsT=a_codes[:, acols].bitcast(FP8X4),
+                        lhsT_scale=a_scales[:, acols],
+                        rhs=q[:, tcols].bitcast(FP8X4),
+                        rhs_scale=sc[:, tcols],
+                        start=(b == 0),
+                        stop=(b == 1),
+                    )
+            zb[pair] = bank
+
+        def add_c(pair):
+            t = zpool.tile([P, 2, 2, P], F32, name="z_s")
+            nc.vector.tensor_tensor(
+                out=t[:],
+                in0=zb[pair][:].rearrange("p h (n q) -> p n h q", n=2),
+                in1=c_t[:].rearrange("p n (h q) -> p n h q", h=2),
+                op=ALU.add,
+            )
+            zs[pair] = t
+
+        def silu_store(pair):
+            o = zpool.tile([P, 2, 256], F32, name="o_t")
+            nc.scalar.activation(out=o[:].rearrange("p n (h q) -> p n h q", h=2), in_=zs[pair][:], func=ACT.Silu)
+            nc.sync.dma_start(out=out[2 * pair : 2 * pair + 2].rearrange("n (m h) q -> m n (h q)", h=2), in_=o[:])
+
+        def prepare_a():
+            for b in range(2):
+                bank = ps_s.tile([P, 4, P], F32, name="s_bank")
+                w = a_raw[:, b, :].bitcast(F32)
+                for h in range(2):
+                    for u in range(2):
+                        nc.tensor.transpose(bank[:, 2 * h + u, :], w[:, 256 * h + u : 256 * (h + 1) : 2], ident[:])
+                dst = a_grp[:].bitcast(F32)[:, 512 * b : 512 * (b + 1)].rearrange("p (h m u) -> p h m u", h=2, u=2)
+                src = bank[:].rearrange("p (h u) m -> p h m u", h=2)
+                if b == 0:
+                    nc.scalar.copy(out=dst, in_=src)
+                else:
+                    nc.vector.tensor_copy(out=dst, in_=src)
+
+        def quantize_a():
+            nc.vector.quantize_mx(out=a_codes[:].bitcast(FP8X4), scales=a_scales[:], in_=a_grp[:])
+
+        interleave_b(1, b2_w)
+        interleave_b(0, b1_raw)
+        quantize_b(1)
+        quantize_b(0)
+        for j in range(NB):
+            for s in range(4):
+                transposes(j, s)
+            unload(j, 0, "S")
+            unload(j, 1, "S")
+            if j + 1 < NB:
+                permute(j + 1)
+            if j >= 6 and j % 2 == 0:
+                silu_store((j - 6) // 2)
+            unload(j, 2, "S")
+            unload(j, 3, "V")
+            if j == 1:
+                prepare_a()
+            quantize_x(j, 0)
+            quantize_x(j, 1)
+            if j == 1:
+                quantize_a()
+            if j >= 5 and j % 2:
+                add_c((j - 5) // 2)
+            if j >= 3 and j % 2:
+                quantize_t((j - 3) // 2)
+            if j >= 4 and j % 2 == 0:
+                stage2((j - 4) // 2)
+            if j:
+                stage1(j - 1, 0)
+                stage1(j - 1, 1)
+                unload1(j - 1, 0, "S")
+                unload1(j - 1, 1, "S")
+        stage2(6)
+        stage1(15, 0)
+        stage1(15, 1)
+        quantize_t_one(14)
+        add_c(6)
+        silu_store(5)
+        unload1(15, 0, "S")
+        unload1(15, 1, "V")
+        silu_store(6)
+        stage2_one(14)
+        quantize_t_one(15)
+        finish_one(14)
+        stage2_one(15)
+        finish_one(15)

@@ -17,13 +17,17 @@ ACT = mybir.ActivationFunctionType
 ALU = mybir.AluOpType
 
 X_BUFS = 16
+FP = (0, 2)
+FQ = (4,)
+CV = (0, 1, 0, 1)
+FV = (0, 0, 0, 0)
 
 
 def tile_ranktwokroneckersumlayer_t_kernel(tc, x, b1, b2_bytes, b2_scale, a1, a2, c, out):
     nc = tc.nc
 
     def permuted_slots(n):
-        return (0, 2)[n] if n < 2 else (4 if n % 2 else 3)
+        return FP[n] if n < len(FP) else FQ[n % len(FQ)]
 
     with ExitStack() as ctx:
         keep = ctx.enter_context(tc.tile_pool(name="keep", bufs=1))
@@ -70,13 +74,15 @@ def tile_ranktwokroneckersumlayer_t_kernel(tc, x, b1, b2_bytes, b2_scale, a1, a2
         nc.sync.dma_start(out=b2_raw[:], in_=b2_bytes.rearrange("(g p t) q -> p g t q", g=2, t=4))
         load_x(0, (1,))
         nc.sync.dma_start(out=b1_raw[:], in_=b1.rearrange("(g p t) q -> p g t q", g=2, t=4))
-        load_x(0, (1, 1, 1))
+        load_x(0, (1, 2))
         load_x(1, (2, 2))
+        load_x(2)
+        load_x(3)
         nc.sync.dma_start(out=a_raw[:, 0, :], in_=a1.rearrange("(m h) k -> m (h k)", h=2))
         nc.sync.dma_start(out=a_raw[:, 1, :], in_=a2.rearrange("(m h) k -> m (h k)", h=2))
         for i in range(2):
             nc.sync.dma_start(out=c_t[:, i, :], in_=c.rearrange("(m h) q -> m (h q)", h=2))
-        for n in range(2, X_BUFS):
+        for n in range(4, X_BUFS):
             load_x(n)
 
         nc.gpsimd.memset(warm[:], 0.0)
@@ -158,15 +164,17 @@ def tile_ranktwokroneckersumlayer_t_kernel(tc, x, b1, b2_bytes, b2_scale, a1, a2
             nc.vector.quantize_mx(out=q[:].bitcast(FP8X4), scales=sc[:], in_=grp[n, h][:])
             codes[n, h] = (q, sc)
 
-        def stage1(n, b):
-            bank = ps_s.tile([P, 4, P], F32, name="s_bank")
-            for t in range(4):
+        def stage1(n, t_major=False):
+            for b in range(2):
+                s1[n, b] = ps_s.tile([P, 4, P], F32, name="s_bank")
+            order = [(b, t) for t in range(4) for b in range(2)] if t_major else [(b, t) for b in range(2) for t in range(4)]
+            for b, t in order:
                 q, sc = codes[n, t // 2]
                 for g in range(2):
                     cols = slice(256 * (t % 2) + 128 * g, 256 * (t % 2) + 128 * (g + 1))
                     bcols = slice(256 * b + 128 * g, 256 * b + 128 * (g + 1))
                     nc.tensor.matmul_mx(
-                        out=bank[:, t, :],
+                        out=s1[n, b][:, t, :],
                         lhsT=q[:, cols].bitcast(FP8X4),
                         lhsT_scale=sc[:, cols],
                         rhs=b_codes[:, bcols].bitcast(FP8X4),
@@ -174,7 +182,6 @@ def tile_ranktwokroneckersumlayer_t_kernel(tc, x, b1, b2_bytes, b2_scale, a1, a2
                         start=(g == 0),
                         stop=(g == 1),
                     )
-            s1[n, b] = bank
 
         def unload1(n, b, eng):
             pair, i = divmod(n, 2)
@@ -296,38 +303,42 @@ def tile_ranktwokroneckersumlayer_t_kernel(tc, x, b1, b2_bytes, b2_scale, a1, a2
             unload(j, 1, "S")
             if j + 1 < NB:
                 permute(j + 1)
-            if j >= 6 and j % 2 == 0:
-                silu_store((j - 6) // 2)
             unload(j, 2, "S")
-            unload(j, 3, "V")
-            if j == 1:
+            unload(j, 3, "V" if CV[j % 4] else "S")
+            if j >= 7 and j % 2:
+                silu_store((j - 7) // 2)
+            if j == 4:
                 prepare_a()
+            if j >= 4 and j % 2 == 0:
+                quantize_t((j - 4) // 2)
             quantize_x(j, 0)
             quantize_x(j, 1)
-            if j == 1:
+            if j == 4:
                 quantize_a()
             if j >= 5 and j % 2:
-                add_c((j - 5) // 2)
-            if j >= 3 and j % 2:
-                quantize_t((j - 3) // 2)
-            if j >= 4 and j % 2 == 0:
-                stage2((j - 4) // 2)
-            if j:
-                stage1(j - 1, 0)
-                stage1(j - 1, 1)
-                unload1(j - 1, 0, "S")
-                unload1(j - 1, 1, "S")
-        stage2(6)
-        stage1(15, 0)
-        stage1(15, 1)
-        quantize_t_one(14)
-        add_c(6)
+                stage2((j - 5) // 2)
+            k = 0 if j == 1 else j - 2
+            if k >= 0 and j != 2:
+                stage1(k)
+                unload1(k, 0, "S")
+                unload1(k, 1, "V" if FV[j % 4] else "S")
+            if j >= 6 and j % 2 == 0:
+                add_c((j - 6) // 2)
+        stage1(14)
+        add_c(5)
+        unload1(14, 0, "S")
+        unload1(14, 1, "V")
+        stage1(15, True)
+        quantize_t(6)
         silu_store(5)
         unload1(15, 0, "S")
         unload1(15, 1, "V")
-        silu_store(6)
+        quantize_t_one(14)
+        stage2(6)
         stage2_one(14)
         quantize_t_one(15)
-        finish_one(14)
+        add_c(6)
         stage2_one(15)
+        finish_one(14)
         finish_one(15)
+        silu_store(6)

@@ -17,8 +17,9 @@ ACT = mybir.ActivationFunctionType
 ALU = mybir.AluOpType
 
 X_BUFS = 16
+WARM = 5
 FP = (0, 2)
-FQ = (4,)
+FQ = (3,)
 CV = (0, 1, 0, 1)
 FV = (0, 0, 0, 0)
 
@@ -87,6 +88,13 @@ def tile_ranktwokroneckersumlayer_t_kernel(tc, x, b1, b2_bytes, b2_scale, a1, a2
 
         nc.gpsimd.memset(warm[:], 0.0)
         make_identity(nc, ident[:])
+        zero = keep.tile([P, 512], BF16, name="zero")
+        nc.vector.memset(zero[:], 0.0)
+        for i in range(WARM):
+            bank = ps_z.tile([P, 2, 256], F32, name="z_bank")
+            nc.tensor.matmul(
+                bank[:].rearrange("p h x -> p (h x)"), lhsT=zero[:, :P], rhs=zero[:], start=True, stop=True
+            )
         nc.scalar.activation(out=warm[:], in_=warm[:], func=ACT.Silu)
 
         for i in range(8):
@@ -327,18 +335,18 @@ def tile_ranktwokroneckersumlayer_t_kernel(tc, x, b1, b2_bytes, b2_scale, a1, a2
         stage1(14)
         add_c(5)
         unload1(14, 0, "S")
+        quantize_t(6)
         unload1(14, 1, "V")
         stage1(15, True)
-        quantize_t(6)
         silu_store(5)
+        stage2(6)
+        quantize_t_one(14)
+        stage2_one(14)
         unload1(15, 0, "S")
         unload1(15, 1, "V")
-        quantize_t_one(14)
-        stage2(6)
-        stage2_one(14)
         quantize_t_one(15)
-        add_c(6)
         stage2_one(15)
+        add_c(6)
+        silu_store(6)
         finish_one(14)
         finish_one(15)
-        silu_store(6)

@@ -19,8 +19,8 @@ ALU = mybir.AluOpType
 X_BUFS = 16
 WARM = 5
 FP = (0, 2)
-FQ = (3,)
-CV = (0, 1, 0, 1)
+FQ = (3, 4)
+CV = (1, 1, 0, 1)
 FV = (0, 0, 0, 0)
 
 
@@ -174,7 +174,10 @@ def tile_ranktwokroneckersumlayer_t_kernel(tc, x, b1, b2_bytes, b2_scale, a1, a2
 
         def stage1(n, t_major=False):
             for b in range(2):
-                s1[n, b] = ps_s.tile([P, 4, P], F32, name="s_bank")
+                if t_major:
+                    s1[n, b] = ps_t.tile([P, 4, P], F32, name="t_bank")
+                else:
+                    s1[n, b] = ps_s.tile([P, 4, P], F32, name="s_bank")
             order = [(b, t) for t in range(4) for b in range(2)] if t_major else [(b, t) for b in range(2) for t in range(4)]
             for b, t in order:
                 q, sc = codes[n, t // 2]
@@ -292,7 +295,7 @@ def tile_ranktwokroneckersumlayer_t_kernel(tc, x, b1, b2_bytes, b2_scale, a1, a2
                         nc.tensor.transpose(bank[:, 2 * h + u, :], w[:, 256 * h + u : 256 * (h + 1) : 2], ident[:])
                 dst = a_grp[:].bitcast(F32)[:, 512 * b : 512 * (b + 1)].rearrange("p (h m u) -> p h m u", h=2, u=2)
                 src = bank[:].rearrange("p (h u) m -> p h m u", h=2)
-                if b == 0:
+                if b < 2:
                     nc.scalar.copy(out=dst, in_=src)
                 else:
                     nc.vector.tensor_copy(out=dst, in_=src)
@@ -305,6 +308,10 @@ def tile_ranktwokroneckersumlayer_t_kernel(tc, x, b1, b2_bytes, b2_scale, a1, a2
         quantize_b(1)
         quantize_b(0)
         for j in range(NB):
+            if j:
+                quantize_x(j - 1, 1)
+            if j == 4:
+                quantize_a()
             for s in range(4):
                 transposes(j, s)
             unload(j, 0, "S")
@@ -312,26 +319,27 @@ def tile_ranktwokroneckersumlayer_t_kernel(tc, x, b1, b2_bytes, b2_scale, a1, a2
             if j + 1 < NB:
                 permute(j + 1)
             unload(j, 2, "S")
-            unload(j, 3, "V" if CV[j % 4] else "S")
+            if not CV[j % 4]:
+                unload(j, 3, "S")
             if j >= 7 and j % 2:
                 silu_store((j - 7) // 2)
-            if j == 4:
+            if j == 2:
                 prepare_a()
             if j >= 4 and j % 2 == 0:
                 quantize_t((j - 4) // 2)
+            if CV[j % 4]:
+                unload(j, 3, "V")
             quantize_x(j, 0)
-            quantize_x(j, 1)
-            if j == 4:
-                quantize_a()
             if j >= 5 and j % 2:
                 stage2((j - 5) // 2)
             k = 0 if j == 1 else j - 2
             if k >= 0 and j != 2:
                 stage1(k)
                 unload1(k, 0, "S")
-                unload1(k, 1, "V" if FV[j % 4] else "S")
+                unload1(k, 1, "S")
             if j >= 6 and j % 2 == 0:
                 add_c((j - 6) // 2)
+        quantize_x(15, 1)
         stage1(14)
         add_c(5)
         unload1(14, 0, "S")

@@ -18,9 +18,10 @@ ALU = mybir.AluOpType
 
 X_BUFS = 16
 WARM = 5
-FP = (0, 2)
+DUMMY = {(0, 3): 2, (2, 3): 2}
+FP = (0, 2, 2, 2)
 FQ = (3, 4)
-CV = (1, 1, 0, 1)
+CV = (1, 0, 1, 0)
 FV = (0, 0, 0, 0)
 
 
@@ -77,8 +78,8 @@ def tile_ranktwokroneckersumlayer_t_kernel(tc, x, b1, b2_bytes, b2_scale, a1, a2
         nc.sync.dma_start(out=b1_raw[:], in_=b1.rearrange("(g p t) q -> p g t q", g=2, t=4))
         load_x(0, (1, 2))
         load_x(1, (2, 2))
-        load_x(2)
-        load_x(3)
+        load_x(2, (2, 2))
+        load_x(3, (2, 2))
         nc.sync.dma_start(out=a_raw[:, 0, :], in_=a1.rearrange("(m h) k -> m (h k)", h=2))
         nc.sync.dma_start(out=a_raw[:, 1, :], in_=a2.rearrange("(m h) k -> m (h k)", h=2))
         for i in range(2):
@@ -90,11 +91,15 @@ def tile_ranktwokroneckersumlayer_t_kernel(tc, x, b1, b2_bytes, b2_scale, a1, a2
         make_identity(nc, ident[:])
         zero = keep.tile([P, 512], BF16, name="zero")
         nc.vector.memset(zero[:], 0.0)
-        for i in range(WARM):
-            bank = ps_z.tile([P, 2, 256], F32, name="z_bank")
-            nc.tensor.matmul(
-                bank[:].rearrange("p h x -> p (h x)"), lhsT=zero[:, :P], rhs=zero[:], start=True, stop=True
-            )
+
+        def warm_tensor(count):
+            for i in range(count):
+                bank = ps_z.tile([P, 2, 256], F32, name="z_bank")
+                nc.tensor.matmul(
+                    bank[:].rearrange("p h x -> p (h x)"), lhsT=zero[:, :P], rhs=zero[:], start=True, stop=True
+                )
+
+        warm_tensor(WARM)
         nc.scalar.activation(out=warm[:], in_=warm[:], func=ACT.Silu)
 
         for i in range(8):
@@ -172,14 +177,15 @@ def tile_ranktwokroneckersumlayer_t_kernel(tc, x, b1, b2_bytes, b2_scale, a1, a2
             nc.vector.quantize_mx(out=q[:].bitcast(FP8X4), scales=sc[:], in_=grp[n, h][:])
             codes[n, h] = (q, sc)
 
-        def stage1(n, t_major=False):
-            for b in range(2):
-                if t_major:
-                    s1[n, b] = ps_t.tile([P, 4, P], F32, name="t_bank")
-                else:
-                    s1[n, b] = ps_s.tile([P, 4, P], F32, name="s_bank")
-            order = [(b, t) for t in range(4) for b in range(2)] if t_major else [(b, t) for b in range(2) for t in range(4)]
-            for b, t in order:
+        def stage1(n, part=None):
+            if part != 1:
+                for b in range(2):
+                    if part == 0:
+                        s1[n, b] = ps_t.tile([P, 4, P], F32, name="t_bank")
+                    else:
+                        s1[n, b] = ps_s.tile([P, 4, P], F32, name="s_bank")
+            ts = range(4) if part is None else (2 * part, 2 * part + 1)
+            for b, t in [(b, t) for b in range(2) for t in ts]:
                 q, sc = codes[n, t // 2]
                 for g in range(2):
                     cols = slice(256 * (t % 2) + 128 * g, 256 * (t % 2) + 128 * (g + 1))
@@ -238,13 +244,16 @@ def tile_ranktwokroneckersumlayer_t_kernel(tc, x, b1, b2_bytes, b2_scale, a1, a2
                     )
             zb[n, "one"] = bank
 
-        def finish_one(n):
+        def add_c_one(n):
             t = zpool.tile([P, 2, P], F32, name="z_one")
             nc.vector.tensor_tensor(
                 out=t[:], in0=zb[n, "one"][:, :2, :], in1=c_t[:, 0, :].rearrange("p (h q) -> p h q", h=2), op=ALU.add
             )
+            zs[n, "one"] = t
+
+        def silu_store_one(n):
             o = zpool.tile([P, 2, P], F32, name="o_one")
-            nc.scalar.activation(out=o[:], in_=t[:], func=ACT.Silu)
+            nc.scalar.activation(out=o[:], in_=zs[n, "one"][:], func=ACT.Silu)
             nc.sync.dma_start(out=out[n].rearrange("(m h) q -> m (h q)", h=2), in_=o[:].rearrange("p h q -> p (h q)"))
 
         def quantize_t(pair):
@@ -307,13 +316,14 @@ def tile_ranktwokroneckersumlayer_t_kernel(tc, x, b1, b2_bytes, b2_scale, a1, a2
         interleave_b(0, b1_raw)
         quantize_b(1)
         quantize_b(0)
-        for j in range(NB):
+        for j in range(NB - 1):
             if j:
                 quantize_x(j - 1, 1)
             if j == 4:
                 quantize_a()
             for s in range(4):
                 transposes(j, s)
+                warm_tensor(DUMMY.get((j, s), 0))
             unload(j, 0, "S")
             unload(j, 1, "S")
             if j + 1 < NB:
@@ -339,22 +349,40 @@ def tile_ranktwokroneckersumlayer_t_kernel(tc, x, b1, b2_bytes, b2_scale, a1, a2
                 unload1(k, 1, "S")
             if j >= 6 and j % 2 == 0:
                 add_c((j - 6) // 2)
+        quantize_x(14, 1)
+        transposes(15, 0)
+        transposes(15, 1)
+        transposes(15, 2)
+        transposes(15, 3)
+        unload(15, 0, "V")
+        unload(15, 1, "S")
+        unload(15, 2, "V")
+        unload(15, 3, "S")
+        stage1(13)
+        quantize_x(15, 0)
+        unload1(13, 0, "S")
         quantize_x(15, 1)
+        unload1(13, 1, "S")
         stage1(14)
-        add_c(5)
-        unload1(14, 0, "S")
         quantize_t(6)
-        unload1(14, 1, "V")
-        stage1(15, True)
-        silu_store(5)
-        stage2(6)
+        unload1(14, 0, "S")
+        unload1(14, 1, "S")
+        stage1(15, 0)
+        stage2(5)
+        stage1(15, 1)
+        silu_store(4)
         quantize_t_one(14)
-        stage2_one(14)
+        add_c(5)
         unload1(15, 0, "S")
+        stage2_one(14)
         unload1(15, 1, "V")
+        stage2(6)
+        add_c_one(14)
+        silu_store(5)
         quantize_t_one(15)
-        stage2_one(15)
         add_c(6)
+        silu_store_one(14)
+        stage2_one(15)
+        add_c_one(15)
         silu_store(6)
-        finish_one(14)
-        finish_one(15)
+        silu_store_one(15)

from contextlib import ExitStack

import concourse.mybir as mybir
from concourse.masks import make_identity

FLOPS = 2 * 16 * 512 * 1024 * 256 + 2 * 2 * 16 * 256 * 512 * 128

P = 128
NB = 16
F32 = mybir.dt.float32
BF16 = mybir.dt.bfloat16
U32 = mybir.dt.uint32
U8 = mybir.dt.uint8
FP8 = mybir.dt.float8_e4m3fn
FP8X4 = mybir.dt.float8_e4m3fn_x4
ACT = mybir.ActivationFunctionType
ALU = mybir.AluOpType

X_BUFS = 16
WARM = 5
DUMMY = {(0, 3): 2, (2, 3): 2}
FP = (0, 2, 2, 2)
FQ = (3, 4)
CV = (1, 0, 1, 0)
FV = (0, 0, 0, 0)


def tile_ranktwokroneckersumlayer_t_kernel(tc, x, b1, b2_bytes, b2_scale, a1, a2, c, out):
    nc = tc.nc

    def permuted_slots(n):
        return FP[n] if n < len(FP) else FQ[n % len(FQ)]

    with ExitStack() as ctx:
        keep = ctx.enter_context(tc.tile_pool(name="keep", bufs=1))
        xpool = ctx.enter_context(tc.tile_pool(name="xpool", bufs=X_BUFS))
        ppool = ctx.enter_context(tc.tile_pool(name="ppool", bufs=2))
        gpool = ctx.enter_context(tc.tile_pool(name="gpool", bufs=4))
        qpool = ctx.enter_context(tc.tile_pool(name="qpool", bufs=6))
        tpool = ctx.enter_context(tc.tile_pool(name="tpool", bufs=2))
        zpool = ctx.enter_context(tc.tile_pool(name="zpool", bufs=3))
        ps_t = ctx.enter_context(tc.psum_pool(name="ps_t", bufs=4))
        ps_s = ctx.enter_context(tc.psum_pool(name="ps_s", bufs=3))
        ps_z = ctx.enter_context(tc.psum_pool(name="ps_z", bufs=1))
        ctx.enter_context(tc.manual_schedule())

        ident = keep.tile([P, P], F32, name="ident")
        warm = keep.tile([P, 1], F32, name="warm")
        b2_raw = keep.tile([P, 2, 4, P], U8, name="b2_raw")
        b2_s = keep.tile([P, 2, 4], F32, name="b2_s")
        b2_w = keep.tile([P, 2, 4, P], BF16, name="b2_w")
        b1_raw = keep.tile([P, 2, 4, P], BF16, name="b1_raw")
        b_grp = keep.tile([P, 2 * 1024], BF16, name="b_grp", align_bytes=64)
        b_codes = keep.tile([P, 512], U32, name="b_codes", align_bytes=64)
        b_scales = keep.tile([P, 512], U8, name="b_scales", align_bytes=64)
        a_raw = keep.tile([P, 2, 1024], BF16, name="a_raw")
        a_grp = keep.tile([P, 2048], BF16, name="a_grp", align_bytes=64)
        a_codes = keep.tile([P, 512], U32, name="a_codes", align_bytes=64)
        a_scales = keep.tile([P, 512], U8, name="a_scales", align_bytes=64)
        c_t = keep.tile([P, 2, 256], BF16, name="c_t")

        xs = {}

        loaded = {}

        def load_x(n, pieces=(4,)):
            if n not in xs:
                xs[n] = xpool.tile([P, 4, 1024], BF16, name="x_t")
            src = x[n].rearrange("(m s) k -> m s k", s=4)
            for step in pieces:
                s = loaded.get(n, 0)
                nc.sync.dma_start(out=xs[n][:, s : s + step, :], in_=src[:, s : s + step, :])
                loaded[n] = s + step

        nc.sync.dma_start(out=b2_s[:], in_=b2_scale.rearrange("(g p t) o -> p g (t o)", g=2, t=4))
        nc.sync.dma_start(out=b2_raw[:], in_=b2_bytes.rearrange("(g p t) q -> p g t q", g=2, t=4))
        load_x(0, (1,))
        nc.sync.dma_start(out=b1_raw[:], in_=b1.rearrange("(g p t) q -> p g t q", g=2, t=4))
        load_x(0, (1, 2))
        load_x(1, (2, 2))
        load_x(2, (2, 2))
        load_x(3, (2, 2))
        nc.sync.dma_start(out=a_raw[:, 0, :], in_=a1.rearrange("(m h) k -> m (h k)", h=2))
        nc.sync.dma_start(out=a_raw[:, 1, :], in_=a2.rearrange("(m h) k -> m (h k)", h=2))
        for i in range(2):
            nc.sync.dma_start(out=c_t[:, i, :], in_=c.rearrange("(m h) q -> m (h q)", h=2))
        for n in range(4, X_BUFS):
            load_x(n)

        nc.gpsimd.memset(warm[:], 0.0)
        make_identity(nc, ident[:])
        zero = keep.tile([P, 512], BF16, name="zero")
        nc.vector.memset(zero[:], 0.0)

        def warm_tensor(count):
            for i in range(count):
                bank = ps_z.tile([P, 2, 256], F32, name="z_bank")
                nc.tensor.matmul(
                    bank[:].rearrange("p h x -> p (h x)"), lhsT=zero[:, :P], rhs=zero[:], start=True, stop=True
                )

        warm_tensor(WARM)
        nc.scalar.activation(out=warm[:], in_=warm[:], func=ACT.Silu)

        for i in range(8):
            g, t = divmod(i, 4)
            src = b2_raw[:, g, t, :].bitcast(FP8)
            if i < 3:
                nc.vector.tensor_scalar(
                    out=b2_w[:, g, t, :], in0=src, scalar1=b2_s[:, g, t : t + 1], scalar2=None, op0=ALU.mult
                )
            else:
                nc.scalar.activation(out=b2_w[:, g, t, :], in_=src, func=ACT.Copy, scale=b2_s[:, g, t : t + 1])

        def interleave_b(i, src):
            nc.vector.tensor_copy(
                out=b_grp[:, 1024 * i : 1024 * (i + 1)].rearrange("p (g q t) -> p g q t", g=2, t=4),
                in_=src[:].rearrange("p g t q -> p g q t"),
            )

        def quantize_b(i):
            nc.vector.quantize_mx(
                out=b_codes[:, 256 * i : 256 * (i + 1)].bitcast(FP8X4),
                scales=b_scales[:, 256 * i : 256 * (i + 1)],
                in_=b_grp[:, 1024 * i : 1024 * (i + 1)],
            )

        perm = {}
        banks = {}
        grp = {}
        codes = {}
        s1 = {}
        tg = {}
        tcodes = {}
        zb = {}
        zs = {}

        def permute(n):
            k = permuted_slots(n)
            if k == 0:
                return
            t = ppool.tile([P, 4096], BF16, name="x_p")
            nc.vector.tensor_copy(
                out=t[:, : 1024 * k].bitcast(F32).rearrange("p (a u w) -> p a u w", u=2, w=P),
                in_=xs[n][:, :k, :].rearrange("p s k -> p (s k)").bitcast(F32).rearrange("p (a w u) -> p a u w", u=2, w=P),
            )
            perm[n] = t

        def transposes(n, s):
            bank = ps_t.tile([P, 4, P], F32, name="t_bank")
            for g in range(2):
                for u in range(2):
                    if s < permuted_slots(n):
                        w = perm[n][:].bitcast(F32)
                        lo = 512 * s + 256 * g + 128 * u
                        src = w[:, lo : lo + 128]
                    else:
                        w = xs[n][:, s, :].bitcast(F32)
                        src = w[:, 256 * g + u : 256 * (g + 1) : 2]
                    nc.tensor.transpose(bank[:, 2 * g + u, :], src, ident[:])
            banks[n, s] = bank

        def unload(n, s, eng):
            h, s2 = divmod(s, 2)
            if s2 == 0:
                grp[n, h] = gpool.tile([P, 2048], BF16, name="x_g", align_bytes=64)
            dst = grp[n, h][:].bitcast(F32)[:, 512 * s2 : 512 * (s2 + 1)].rearrange("p (g m u) -> p g m u", g=2, u=2)
            src = banks[n, s][:].rearrange("p (g u) m -> p g m u", g=2)
            if eng == "S":
                nc.scalar.copy(out=dst, in_=src)
            else:
                nc.vector.tensor_copy(out=dst, in_=src)

        def quantize_x(n, h):
            q = qpool.tile([P, 512], U32, name="x_q", align_bytes=64)
            sc = qpool.tile([P, 512], U8, name="x_s", align_bytes=64)
            nc.vector.quantize_mx(out=q[:].bitcast(FP8X4), scales=sc[:], in_=grp[n, h][:])
            codes[n, h] = (q, sc)

        def stage1(n, part=None):
            if part != 1:
                for b in range(2):
                    if part == 0:
                        s1[n, b] = ps_t.tile([P, 4, P], F32, name="t_bank")
                    else:
                        s1[n, b] = ps_s.tile([P, 4, P], F32, name="s_bank")
            ts = range(4) if part is None else (2 * part, 2 * part + 1)
            for b, t in [(b, t) for b in range(2) for t in ts]:
                q, sc = codes[n, t // 2]
                for g in range(2):
                    cols = slice(256 * (t % 2) + 128 * g, 256 * (t % 2) + 128 * (g + 1))
                    bcols = slice(256 * b + 128 * g, 256 * b + 128 * (g + 1))
                    nc.tensor.matmul_mx(
                        out=s1[n, b][:, t, :],
                        lhsT=q[:, cols].bitcast(FP8X4),
                        lhsT_scale=sc[:, cols],
                        rhs=b_codes[:, bcols].bitcast(FP8X4),
                        rhs_scale=b_scales[:, bcols],
                        start=(g == 0),
                        stop=(g == 1),
                    )

        def unload1(n, b, eng):
            pair, i = divmod(n, 2)
            if i == 0 and b == 0:
                tg[pair] = tpool.tile([P, 2048], BF16, name="t_g", align_bytes=64)
            lo = 512 * (2 * b + i)
            dst = tg[pair][:, lo : lo + 512].rearrange("p (q t) -> p q t", t=4)
            src = s1[n, b][:].rearrange("p t q -> p q t")
            if eng == "S":
                nc.scalar.copy(out=dst, in_=src)
            else:
                nc.vector.tensor_copy(out=dst, in_=src)

        def quantize_t_one(n):
            pair, i = divmod(n, 2)
            if i == 0:
                q = tpool.tile([P, 512], U32, name="t_q", align_bytes=64)
                sc = tpool.tile([P, 512], U8, name="t_s", align_bytes=64)
                tcodes[pair] = (q, sc)
            q, sc = tcodes[pair]
            for b in range(2):
                lo = 128 * (2 * b + i)
                nc.vector.quantize_mx(
                    out=q[:, lo : lo + 128].bitcast(FP8X4), scales=sc[:, lo : lo + 128], in_=tg[pair][:, 4 * lo : 4 * lo + 512]
                )

        def stage2_one(n):
            pair, i = divmod(n, 2)
            bank = ps_t.tile([P, 4, P], F32, name="t_bank")
            q, sc = tcodes[pair]
            for h in range(2):
                for b in range(2):
                    acols = slice(128 * (2 * b + h), 128 * (2 * b + h + 1))
                    tcols = slice(128 * (2 * b + i), 128 * (2 * b + i + 1))
                    nc.tensor.matmul_mx(
                        out=bank[:, h, :],
                        lhsT=a_codes[:, acols].bitcast(FP8X4),
                        lhsT_scale=a_scales[:, acols],
                        rhs=q[:, tcols].bitcast(FP8X4),
                        rhs_scale=sc[:, tcols],
                        start=(b == 0),
                        stop=(b == 1),
                    )
            zb[n, "one"] = bank

        def add_c_one(n):
            t = zpool.tile([P, 2, P], F32, name="z_one")
            nc.vector.tensor_tensor(
                out=t[:], in0=zb[n, "one"][:, :2, :], in1=c_t[:, 0, :].rearrange("p (h q) -> p h q", h=2), op=ALU.add
            )
            zs[n, "one"] = t

        def silu_store_one(n):
            o = zpool.tile([P, 2, P], F32, name="o_one")
            nc.scalar.activation(out=o[:], in_=zs[n, "one"][:], func=ACT.Silu)
            nc.sync.dma_start(out=out[n].rearrange("(m h) q -> m (h q)", h=2), in_=o[:].rearrange("p h q -> p (h q)"))

        def quantize_t(pair):
            q = tpool.tile([P, 512], U32, name="t_q", align_bytes=64)
            sc = tpool.tile([P, 512], U8, name="t_s", align_bytes=64)
            nc.vector.quantize_mx(out=q[:].bitcast(FP8X4), scales=sc[:], in_=tg[pair][:])
            tcodes[pair] = (q, sc)

        def stage2(pair):
            bank = ps_z.tile([P, 2, 256], F32, name="z_bank")
            q, sc = tcodes[pair]
            for h in range(2):
                for b in range(2):
                    acols = slice(128 * (2 * b + h), 128 * (2 * b + h + 1))
                    tcols = slice(256 * b, 256 * (b + 1))
                    nc.tensor.matmul_mx(
                        out=bank[:, h, :],
                        lhsT=a_codes[:, acols].bitcast(FP8X4),
                        lhsT_scale=a_scales[:, acols],
                        rhs=q[:, tcols].bitcast(FP8X4),
                        rhs_scale=sc[:, tcols],
                        start=(b == 0),
                        stop=(b == 1),
                    )
            zb[pair] = bank

        def add_c(pair):
            t = zpool.tile([P, 2, 2, P], F32, name="z_s")
            nc.vector.tensor_tensor(
                out=t[:],
                in0=zb[pair][:].rearrange("p h (n q) -> p n h q", n=2),
                in1=c_t[:].rearrange("p n (h q) -> p n h q", h=2),
                op=ALU.add,
            )
            zs[pair] = t

        def silu_store(pair):
            o = zpool.tile([P, 2, 256], F32, name="o_t")
            nc.scalar.activation(out=o[:].rearrange("p n (h q) -> p n h q", h=2), in_=zs[pair][:], func=ACT.Silu)
            nc.sync.dma_start(out=out[2 * pair : 2 * pair + 2].rearrange("n (m h) q -> m n (h q)", h=2), in_=o[:])

        def prepare_a():
            for b in range(2):
                bank = ps_s.tile([P, 4, P], F32, name="s_bank")
                w = a_raw[:, b, :].bitcast(F32)
                for h in range(2):
                    for u in range(2):
                        nc.tensor.transpose(bank[:, 2 * h + u, :], w[:, 256 * h + u : 256 * (h + 1) : 2], ident[:])
                dst = a_grp[:].bitcast(F32)[:, 512 * b : 512 * (b + 1)].rearrange("p (h m u) -> p h m u", h=2, u=2)
                src = bank[:].rearrange("p (h u) m -> p h m u", h=2)
                if b < 2:
                    nc.scalar.copy(out=dst, in_=src)
                else:
                    nc.vector.tensor_copy(out=dst, in_=src)

        def quantize_a():
            nc.vector.quantize_mx(out=a_codes[:].bitcast(FP8X4), scales=a_scales[:], in_=a_grp[:])

        interleave_b(1, b2_w)
        interleave_b(0, b1_raw)
        quantize_b(1)
        quantize_b(0)
        for j in range(NB - 1):
            if j:
                quantize_x(j - 1, 1)
            if j == 4:
                quantize_a()
            for s in range(4):
                transposes(j, s)
                warm_tensor(DUMMY.get((j, s), 0))
            unload(j, 0, "S")
            unload(j, 1, "S")
            if j + 1 < NB:
                permute(j + 1)
            unload(j, 2, "S")
            if not CV[j % 4]:
                unload(j, 3, "S")
            if j >= 7 and j % 2:
                silu_store((j - 7) // 2)
            if j == 2:
                prepare_a()
            if j >= 4 and j % 2 == 0:
                quantize_t((j - 4) // 2)
            if CV[j % 4]:
                unload(j, 3, "V")
            quantize_x(j, 0)
            if j >= 5 and j % 2:
                stage2((j - 5) // 2)
            k = 0 if j == 1 else j - 2
            if k >= 0 and j != 2:
                stage1(k)
                unload1(k, 0, "S")
                unload1(k, 1, "S")
            if j >= 6 and j % 2 == 0:
                add_c((j - 6) // 2)
        quantize_x(14, 1)
        transposes(15, 0)
        transposes(15, 1)
        transposes(15, 2)
        transposes(15, 3)
        unload(15, 0, "V")
        unload(15, 1, "S")
        unload(15, 2, "V")
        unload(15, 3, "S")
        stage1(13)
        quantize_x(15, 0)
        unload1(13, 0, "S")
        quantize_x(15, 1)
        unload1(13, 1, "S")
        stage1(14)
        quantize_t(6)
        unload1(14, 0, "S")
        unload1(14, 1, "S")
        stage1(15, 0)
        stage2(5)
        stage1(15, 1)
        silu_store(4)
        quantize_t_one(14)
        add_c(5)
        unload1(15, 0, "S")
        stage2_one(14)
        unload1(15, 1, "V")
        stage2(6)
        add_c_one(14)
        silu_store(5)
        quantize_t_one(15)
        add_c(6)
        silu_store_one(14)
        stage2_one(15)
        add_c_one(15)
        silu_store(6)
        silu_store_one(15)
